import numpy as np
import ml_dtypes


def mxq(x, axis, fmt="e4m3"):
    dtype, down = {"e4m3": (ml_dtypes.float8_e4m3fn, 7), "e5m2": (ml_dtypes.float8_e5m2, 14)}[fmt]
    v = np.moveaxis(np.asarray(x, np.float32).astype(ml_dtypes.bfloat16).astype(np.float64), axis, -1)
    blocks = v.reshape(v.shape[:-1] + (-1, 32))
    amax = np.abs(blocks).max(-1, keepdims=True)
    byte = np.maximum(np.where(amax > 0, np.frexp(amax)[1] - 1 + 127, 0) - down, 1)
    scale = np.exp2(byte - 127.0)
    codes = (blocks / scale).astype(np.float32).astype(dtype).astype(np.float64)
    return np.moveaxis((codes * scale).reshape(v.shape), -1, axis)


WIDE = False


def mx_kscale(k):
    if not WIDE:
        return np.ones(k)
    levels = np.array([10, -10, 5, -5, 0])
    if k % 512:
        return np.exp2(np.random.permutation(np.resize(levels, k // 32))).repeat(32)
    a = np.empty((k // 512, 16))
    for p in range(k // 512):
        a[p, :8] = np.random.permutation(np.resize(levels, 8))
        for g in range(8):
            far = levels[np.abs(levels - a[p, g]) >= 10]
            a[p, g + 8] = far[np.random.randint(len(far))]
    return np.exp2(a.ravel()).repeat(32)


def f64(x):
    return np.asarray(x).astype(np.float64)


def striped(idx):
    return np.tile(idx.reshape(-1, 16).T, (8, 1)).astype(np.uint16)


def unstriped(offs):
    return offs[:16].T.reshape(-1).astype(np.int64)


def pack_weight(w):
    k, n = w.shape
    w = f64(np.asarray(w, np.float32).astype(ml_dtypes.bfloat16)).reshape(k // 32, 32, n)
    amax = np.abs(w).max(1)
    byte = np.clip(np.where(amax > 0, np.frexp(amax)[1] - 1 + 127 - 7, 1), 1, 254)
    scaled = (w * np.exp2(127.0 - byte)[:, None, :]).reshape(k, n).astype(np.float32)
    words = np.ascontiguousarray(scaled.reshape(k // 512, 128, 4, n).transpose(0, 1, 3, 2)).astype(ml_dtypes.float8_e4m3fn).view(np.uint8)
    return words, np.ascontiguousarray(byte.astype(np.uint8).reshape(k // 512, 16, n))


def unpack_weight(words, scales):
    g, p, n, _ = words.shape
    vals = np.ascontiguousarray(words).view(ml_dtypes.float8_e4m3fn).astype(np.float64) * np.repeat(np.exp2(scales.astype(np.float64) - 127.0), 8, axis=1)[..., None]
    return vals.transpose(0, 1, 3, 2).reshape(g * 512, n)


def relu(v):
    return np.maximum(v, 0.0)


K, T, E, C, N = 1024, 2048, 16, 128, 128


def by_expert(wq, xq):
    return np.concatenate([wq[e].T @ xq[:, e * C:(e + 1) * C] for e in range(E)], axis=1)


def setup_inputs():
    n = np.random.standard_normal
    s = mx_kscale(K)[:, None]
    packed = [pack_weight(m) for m in n((E, K, N)) / np.sqrt(K) / s[None]]
    return {
        "xT": (n((K, T)) * s).astype(np.float32),
        "w_words": np.stack([m[0] for m in packed]),
        "w_scales": np.stack([m[1] for m in packed]),
        "b": (0.3 * n((N, E))).astype(np.float32),
        "gate": np.tile(np.random.uniform(0.2, 1.0, E * C), (N, 1)).astype(np.float32),
        "offs": striped(np.random.permutation(T)[:E * C]),
    }


def reference(xT, w_words, w_scales, b, gate, offs):
    idx = unstriped(offs)
    xq = mxq(f64(xT)[:, idx], 0, "e4m3")
    w = np.stack([unpack_weight(w_words[e], w_scales[e]) for e in range(E)])
    y = by_expert(w, xq)
    y = relu(y + np.repeat(f64(b), C, axis=1))
    out = np.zeros((N, T))
    out[:, idx] = f64(gate) * y
    return out

@@ -1,0 +1,152 @@
+from contextlib import ExitStack
+
+import concourse.mybir as mybir
+
+K, T, E, C, N = 1024, 2048, 16, 128, 128
+FLOPS = 2 * K * N * E * C
+
+F32 = mybir.dt.float32
+BF16 = mybir.dt.bfloat16
+I32 = mybir.dt.int32
+U32 = mybir.dt.uint32
+U16 = mybir.dt.uint16
+U8 = mybir.dt.uint8
+FP8X4 = mybir.dt.float8_e4m3fn_x4
+RELU = mybir.ActivationFunctionType.Relu
+MULT = mybir.AluOpType.mult
+
+P = 128
+PASSES = K // 512
+SLOTS = E * C
+
+LOADS = (
+    (0, 0, 256),
+    (0, 256, 256),
+    (0, 512, 512),
+    (0, 1024, 512),
+    (0, 1536, 512),
+    (1, 0, 512),
+    (1, 512, 512),
+    (1, 1024, 512),
+    (1, 1536, 256),
+    (1, 1792, 256),
+)
+PIECES = (
+    (0, 0, 0, 256, "s"),
+    (0, 1, 0, 256, "v"),
+    (0, 2, 0, 512, "s"),
+    (0, 3, 0, 512, "v"),
+    (0, 4, 0, 256, "s"),
+    (0, 4, 256, 256, "v"),
+    (1, 5, 0, 512, "s"),
+    (1, 6, 0, 512, "s"),
+    (1, 7, 0, 256, "s"),
+    (1, 7, 256, 256, "v"),
+    (1, 8, 0, 256, "s"),
+    (1, 9, 0, 256, "v"),
+)
+CUTS = ((0, 1024), (1024, 2048))
+
+
+def tile_routed_moe_kernel(tc, xT, w_words, w_scales, b, gate, offs, out):
+    nc = tc.nc
+    with ExitStack() as ctx:
+        keep = ctx.enter_context(tc.tile_pool(name="keep", bufs=1))
+        psum = ctx.enter_context(tc.psum_pool(name="psum", bufs=1))
+
+        lst = keep.tile([P, SLOTS // 16], U16, name="lst")
+        nc.sync.dma_start(lst[:], offs)
+        b_sb = keep.tile([P, E], F32, name="b_sb")
+        nc.scalar.dma_start(out=b_sb[:], in_=b)
+
+        xs = keep.tile([P, T], U8, name="xs", align_bytes=64)
+        nc.gpsimd.memset(xs[:], 0)
+        ws = keep.tile([P, E, N], U8, name="ws", align_bytes=64)
+        nc.gpsimd.memset(ws[:].rearrange("p e n -> p (e n)").bitcast(I32), 0)
+
+        x_view = xT.rearrange("(g p t) n -> g p t n", p=P, t=4)
+        raws = []
+        for i, (g, t0, n) in enumerate(LOADS):
+            raw = keep.tile([P, 4, n], F32, name="raw%d" % i)
+            nc.sync.dma_start(out=raw[:], in_=x_view[g, :, :, t0 : t0 + n])
+            raws.append(raw)
+
+        for a in range(PASSES):
+            for q in range(4):
+                nc.sync.dma_start(
+                    out=ws[32 * q + 4 * a : 32 * q + 4 * a + 4, :, :].bitcast(I32),
+                    in_=w_scales[:, a, 4 * q : 4 * q + 4, :].rearrange("e q n -> q e n").bitcast(I32),
+                )
+        ww = keep.tile([P, E * PASSES, N], U32, name="ww", align_bytes=64)
+        w_view = w_words.rearrange("e a p n r -> p (e a) (n r)").bitcast(I32)
+        for h in range(2):
+            rows = slice(h * E, (h + 1) * E)
+            nc.sync.dma_start(out=ww[:, rows, :].bitcast(I32), in_=w_view[:, rows, :])
+        gate_sb = keep.tile([P, SLOTS], F32, name="gate_sb")
+        nc.sync.dma_start(out=gate_sb[:], in_=gate)
+
+        words = [keep.tile([P, T], U32, name="words%d" % g, align_bytes=64) for g in range(PASSES)]
+        gw = [keep.tile([P, SLOTS], U32, name="gw%d" % g, align_bytes=64) for g in range(PASSES)]
+        gs = keep.tile([P, SLOTS], U8, name="gs", align_bytes=64)
+
+        def quantise(i):
+            g, load, first, n, eng = PIECES[i]
+            t0 = LOADS[load][1] + first
+            inter = keep.tile([P, n, 4], BF16, name="inter%d" % i, align_bytes=64)
+            src = raws[load][:, :, first : first + n].rearrange("p t n -> p n t")
+            if eng == "s":
+                nc.scalar.copy(out=inter[:], in_=src)
+            else:
+                nc.vector.tensor_copy(out=inter[:], in_=src)
+            nc.vector.quantize_mx(
+                out=words[g][:, t0 : t0 + n].bitcast(FP8X4),
+                scales=xs[4 * g : P, t0 : t0 + n],
+                in_=inter[:].rearrange("p n t -> p (n t)"),
+            )
+
+        def gather_words(g, lo, hi):
+            nc.vector.tensor_copy(out=gw[g][:, lo:hi], in_=words[g][:].indirect(lst[:, lo // 16 : hi // 16]))
+
+        def gather_scales(lo, hi):
+            nc.vector.tensor_copy(out=gs[:, lo:hi], in_=xs[:].indirect(lst[:, lo // 16 : hi // 16]))
+
+        for i in range(len(PIECES)):
+            if PIECES[i][0] == 0:
+                quantise(i)
+        for lo, hi in CUTS:
+            gather_words(0, lo, hi)
+        for i in range(len(PIECES)):
+            if PIECES[i][0] == 1:
+                quantise(i)
+
+        y = keep.tile([P, SLOTS], F32, name="y")
+        for lo, hi in CUTS:
+            gather_words(1, lo, hi)
+            gather_scales(lo, hi)
+            for e0 in range(lo // C, hi // C, 2):
+                acc = psum.tile([P, 2 * C], F32, name="acc%d" % e0)
+                for j in range(2):
+                    e = e0 + j
+                    sl = slice(e * C, (e + 1) * C)
+                    for g in range(PASSES):
+                        nc.tensor.matmul_mx(
+                            out=acc[:, j * C : (j + 1) * C],
+                            lhsT=ww[:, PASSES * e + g, :].bitcast(FP8X4),
+                            lhsT_scale=ws[4 * g : P, e, :],
+                            rhs=gw[g][:, sl].bitcast(FP8X4),
+                            rhs_scale=gs[4 * g : P, sl],
+                            start=(g == 0),
+                            stop=(g == PASSES - 1),
+                        )
+                for j in range(2):
+                    e = e0 + j
+                    nc.scalar.activation(
+                        y[:, e * C : (e + 1) * C], acc[:, j * C : (j + 1) * C], RELU, bias=b_sb[:, e : e + 1]
+                    )
+
+        z = keep.tile([P, SLOTS], F32, name="z")
+        out_sb = keep.tile([P, T], F32, name="out_sb")
+        for lo, hi in CUTS:
+            nc.vector.tensor_tensor(z[:, lo:hi], y[:, lo:hi], gate_sb[:, lo:hi], MULT)
+            nc.vector.tensor_copy(out_sb[:].indirect(lst[:, lo // 16 : hi // 16]), z[:, lo:hi])
+        nc.sync.dma_start(out=out, in_=out_sb[:])

@@ -93,11 +93,12 @@ def tile_routed_moe_kernel(tc, xT, w_words, w_scales, b, gate, offs, out):
             g, load, first, n, eng = PIECES[i]
             t0 = LOADS[load][1] + first
             inter = keep.tile([P, n, 4], BF16, name="inter%d" % i, align_bytes=64)
-            src = raws[load][:, :, first : first + n].rearrange("p t n -> p n t")
+            dst = inter[:].rearrange("p (c i) t -> p c t i", i=4)
+            src = raws[load][:, :, first : first + n].rearrange("p t (c i) -> p c t i", i=4)
             if eng == "s":
-                nc.scalar.copy(out=inter[:], in_=src)
+                nc.scalar.copy(out=dst, in_=src)
             else:
-                nc.vector.tensor_copy(out=inter[:], in_=src)
+                nc.vector.tensor_copy(out=dst, in_=src)
             nc.vector.quantize_mx(
                 out=words[g][:, t0 : t0 + n].bitcast(FP8X4),
                 scales=xs[4 * g : P, t0 : t0 + n],
@@ -144,9 +145,9 @@ def tile_routed_moe_kernel(tc, xT, w_words, w_scales, b, gate, offs, out):
                         y[:, e * C : (e + 1) * C], acc[:, j * C : (j + 1) * C], RELU, bias=b_sb[:, e : e + 1]
                     )
 
-        z = keep.tile([P, SLOTS], F32, name="z")
         out_sb = keep.tile([P, T], F32, name="out_sb")
         for lo, hi in CUTS:
-            nc.vector.tensor_tensor(z[:, lo:hi], y[:, lo:hi], gate_sb[:, lo:hi], MULT)
-            nc.vector.tensor_copy(out_sb[:].indirect(lst[:, lo // 16 : hi // 16]), z[:, lo:hi])
+            nc.vector.tensor_tensor(
+                out_sb[:].indirect(lst[:, lo // 16 : hi // 16]), y[:, lo:hi], gate_sb[:, lo:hi], MULT
+            )
         nc.sync.dma_start(out=out, in_=out_sb[:])

@@ -20,30 +20,28 @@ PASSES = K // 512
 SLOTS = E * C
 
 LOADS = (
-    (0, 0, 256),
-    (0, 256, 256),
-    (0, 512, 512),
+    (0, 0, 1024),
     (0, 1024, 512),
     (0, 1536, 512),
     (1, 0, 512),
     (1, 512, 512),
     (1, 1024, 512),
-    (1, 1536, 256),
-    (1, 1792, 256),
+    (1, 1536, 384),
+    (1, 1920, 128),
 )
 PIECES = (
-    (0, 0, 0, 256, "s"),
-    (0, 1, 0, 256, "v"),
-    (0, 2, 0, 512, "s"),
-    (0, 3, 0, 512, "v"),
-    (0, 4, 0, 256, "s"),
-    (0, 4, 256, 256, "v"),
-    (1, 5, 0, 512, "s"),
-    (1, 6, 0, 512, "s"),
-    (1, 7, 0, 256, "s"),
-    (1, 7, 256, 256, "v"),
-    (1, 8, 0, 256, "s"),
-    (1, 9, 0, 256, "v"),
+    (0, 0, 0, 512, "s"),
+    (0, 0, 512, 512, "v"),
+    (0, 1, 0, 512, "v"),
+    (0, 2, 0, 256, "s"),
+    (0, 2, 256, 256, "v"),
+    (1, 3, 0, 512, "s"),
+    (1, 4, 0, 512, "s"),
+    (1, 5, 0, 256, "s"),
+    (1, 5, 256, 256, "v"),
+    (1, 6, 0, 256, "v"),
+    (1, 6, 256, 128, "s"),
+    (1, 7, 0, 128, "s"),
 )
 CUTS = ((0, 1024), (1024, 2048))
 
@@ -55,9 +53,7 @@ def tile_routed_moe_kernel(tc, xT, w_words, w_scales, b, gate, offs, out):
         psum = ctx.enter_context(tc.psum_pool(name="psum", bufs=1))
 
         lst = keep.tile([P, SLOTS // 16], U16, name="lst")
-        nc.sync.dma_start(lst[:], offs)
         b_sb = keep.tile([P, E], F32, name="b_sb")
-        nc.scalar.dma_start(out=b_sb[:], in_=b)
 
         xs = keep.tile([P, T], U8, name="xs", align_bytes=64)
         nc.gpsimd.memset(xs[:], 0)
@@ -70,6 +66,8 @@ def tile_routed_moe_kernel(tc, xT, w_words, w_scales, b, gate, offs, out):
             raw = keep.tile([P, 4, n], F32, name="raw%d" % i)
             nc.sync.dma_start(out=raw[:], in_=x_view[g, :, :, t0 : t0 + n])
             raws.append(raw)
+            if i == 0:
+                nc.sync.dma_start(lst[:], offs)
 
         for a in range(PASSES):
             for q in range(4):
@@ -79,11 +77,14 @@ def tile_routed_moe_kernel(tc, xT, w_words, w_scales, b, gate, offs, out):
                 )
         ww = keep.tile([P, E * PASSES, N], U32, name="ww", align_bytes=64)
         w_view = w_words.rearrange("e a p n r -> p (e a) (n r)").bitcast(I32)
+        gate_sb = keep.tile([P, SLOTS], F32, name="gate_sb")
         for h in range(2):
             rows = slice(h * E, (h + 1) * E)
             nc.sync.dma_start(out=ww[:, rows, :].bitcast(I32), in_=w_view[:, rows, :])
-        gate_sb = keep.tile([P, SLOTS], F32, name="gate_sb")
-        nc.sync.dma_start(out=gate_sb[:], in_=gate)
+            if h == 0:
+                nc.sync.dma_start(out=b_sb[:], in_=b)
+            cols = slice(h * SLOTS // 2, (h + 1) * SLOTS // 2)
+            nc.sync.dma_start(out=gate_sb[:, cols], in_=gate[:, cols])
 
         words = [keep.tile([P, T], U32, name="words%d" % g, align_bytes=64) for g in range(PASSES)]
         gw = [keep.tile([P, SLOTS], U32, name="gw%d" % g, align_bytes=64) for g in range(PASSES)]

@@ -31,17 +31,18 @@ LOADS = (
 )
 PIECES = (
     (0, 0, 0, 512, "s"),
-    (0, 0, 512, 512, "v"),
+    (0, 0, 512, 256, "v"),
+    (0, 0, 768, 256, "s"),
     (0, 1, 0, 512, "v"),
     (0, 2, 0, 256, "s"),
     (0, 2, 256, 256, "v"),
     (1, 3, 0, 512, "s"),
     (1, 4, 0, 512, "s"),
     (1, 5, 0, 256, "s"),
-    (1, 5, 256, 256, "v"),
+    (1, 5, 256, 256, "s"),
     (1, 6, 0, 256, "v"),
     (1, 6, 256, 128, "s"),
-    (1, 7, 0, 128, "s"),
+    (1, 7, 0, 128, "v"),
 )
 CUTS = ((0, 1024), (1024, 2048))
 

from contextlib import ExitStack

import concourse.mybir as mybir

K, T, E, C, N = 1024, 2048, 16, 128, 128
FLOPS = 2 * K * N * E * C

F32 = mybir.dt.float32
BF16 = mybir.dt.bfloat16
I32 = mybir.dt.int32
U32 = mybir.dt.uint32
U16 = mybir.dt.uint16
U8 = mybir.dt.uint8
FP8X4 = mybir.dt.float8_e4m3fn_x4
RELU = mybir.ActivationFunctionType.Relu
MULT = mybir.AluOpType.mult

P = 128
PASSES = K // 512
SLOTS = E * C

LOADS = (
    (0, 0, 1024),
    (0, 1024, 512),
    (0, 1536, 512),
    (1, 0, 512),
    (1, 512, 512),
    (1, 1024, 512),
    (1, 1536, 384),
    (1, 1920, 128),
)
PIECES = (
    (0, 0, 0, 512, "s"),
    (0, 0, 512, 256, "v"),
    (0, 0, 768, 256, "s"),
    (0, 1, 0, 512, "v"),
    (0, 2, 0, 256, "s"),
    (0, 2, 256, 256, "v"),
    (1, 3, 0, 512, "s"),
    (1, 4, 0, 512, "s"),
    (1, 5, 0, 256, "s"),
    (1, 5, 256, 256, "s"),
    (1, 6, 0, 256, "v"),
    (1, 6, 256, 128, "s"),
    (1, 7, 0, 128, "v"),
)
CUTS = ((0, 1024), (1024, 2048))


def tile_routed_moe_kernel(tc, xT, w_words, w_scales, b, gate, offs, out):
    nc = tc.nc
    with ExitStack() as ctx:
        keep = ctx.enter_context(tc.tile_pool(name="keep", bufs=1))
        psum = ctx.enter_context(tc.psum_pool(name="psum", bufs=1))

        lst = keep.tile([P, SLOTS // 16], U16, name="lst")
        b_sb = keep.tile([P, E], F32, name="b_sb")

        xs = keep.tile([P, T], U8, name="xs", align_bytes=64)
        nc.gpsimd.memset(xs[:], 0)
        ws = keep.tile([P, E, N], U8, name="ws", align_bytes=64)
        nc.gpsimd.memset(ws[:].rearrange("p e n -> p (e n)").bitcast(I32), 0)

        x_view = xT.rearrange("(g p t) n -> g p t n", p=P, t=4)
        raws = []
        for i, (g, t0, n) in enumerate(LOADS):
            raw = keep.tile([P, 4, n], F32, name="raw%d" % i)
            nc.sync.dma_start(out=raw[:], in_=x_view[g, :, :, t0 : t0 + n])
            raws.append(raw)
            if i == 0:
                nc.sync.dma_start(lst[:], offs)

        for a in range(PASSES):
            for q in range(4):
                nc.sync.dma_start(
                    out=ws[32 * q + 4 * a : 32 * q + 4 * a + 4, :, :].bitcast(I32),
                    in_=w_scales[:, a, 4 * q : 4 * q + 4, :].rearrange("e q n -> q e n").bitcast(I32),
                )
        ww = keep.tile([P, E * PASSES, N], U32, name="ww", align_bytes=64)
        w_view = w_words.rearrange("e a p n r -> p (e a) (n r)").bitcast(I32)
        gate_sb = keep.tile([P, SLOTS], F32, name="gate_sb")
        for h in range(2):
            rows = slice(h * E, (h + 1) * E)
            nc.sync.dma_start(out=ww[:, rows, :].bitcast(I32), in_=w_view[:, rows, :])
            if h == 0:
                nc.sync.dma_start(out=b_sb[:], in_=b)
            cols = slice(h * SLOTS // 2, (h + 1) * SLOTS // 2)
            nc.sync.dma_start(out=gate_sb[:, cols], in_=gate[:, cols])

        words = [keep.tile([P, T], U32, name="words%d" % g, align_bytes=64) for g in range(PASSES)]
        gw = [keep.tile([P, SLOTS], U32, name="gw%d" % g, align_bytes=64) for g in range(PASSES)]
        gs = keep.tile([P, SLOTS], U8, name="gs", align_bytes=64)

        def quantise(i):
            g, load, first, n, eng = PIECES[i]
            t0 = LOADS[load][1] + first
            inter = keep.tile([P, n, 4], BF16, name="inter%d" % i, align_bytes=64)
            dst = inter[:].rearrange("p (c i) t -> p c t i", i=4)
            src = raws[load][:, :, first : first + n].rearrange("p t (c i) -> p c t i", i=4)
            if eng == "s":
                nc.scalar.copy(out=dst, in_=src)
            else:
                nc.vector.tensor_copy(out=dst, in_=src)
            nc.vector.quantize_mx(
                out=words[g][:, t0 : t0 + n].bitcast(FP8X4),
                scales=xs[4 * g : P, t0 : t0 + n],
                in_=inter[:].rearrange("p n t -> p (n t)"),
            )

        def gather_words(g, lo, hi):
            nc.vector.tensor_copy(out=gw[g][:, lo:hi], in_=words[g][:].indirect(lst[:, lo // 16 : hi // 16]))

        def gather_scales(lo, hi):
            nc.vector.tensor_copy(out=gs[:, lo:hi], in_=xs[:].indirect(lst[:, lo // 16 : hi // 16]))

        for i in range(len(PIECES)):
            if PIECES[i][0] == 0:
                quantise(i)
        for lo, hi in CUTS:
            gather_words(0, lo, hi)
        for i in range(len(PIECES)):
            if PIECES[i][0] == 1:
                quantise(i)

        y = keep.tile([P, SLOTS], F32, name="y")
        for lo, hi in CUTS:
            gather_words(1, lo, hi)
            gather_scales(lo, hi)
            for e0 in range(lo // C, hi // C, 2):
                acc = psum.tile([P, 2 * C], F32, name="acc%d" % e0)
                for j in range(2):
                    e = e0 + j
                    sl = slice(e * C, (e + 1) * C)
                    for g in range(PASSES):
                        nc.tensor.matmul_mx(
                            out=acc[:, j * C : (j + 1) * C],
                            lhsT=ww[:, PASSES * e + g, :].bitcast(FP8X4),
                            lhsT_scale=ws[4 * g : P, e, :],
                            rhs=gw[g][:, sl].bitcast(FP8X4),
                            rhs_scale=gs[4 * g : P, sl],
                            start=(g == 0),
                            stop=(g == PASSES - 1),
                        )
                for j in range(2):
                    e = e0 + j
                    nc.scalar.activation(
                        y[:, e * C : (e + 1) * C], acc[:, j * C : (j + 1) * C], RELU, bias=b_sb[:, e : e + 1]
                    )

        out_sb = keep.tile([P, T], F32, name="out_sb")
        for lo, hi in CUTS:
            nc.vector.tensor_tensor(
                out_sb[:].indirect(lst[:, lo // 16 : hi // 16]), y[:, lo:hi], gate_sb[:, lo:hi], MULT
            )
        nc.sync.dma_start(out=out, in_=out_sb[:])
